import numpy as np
import ml_dtypes


def mxq(x, axis, fmt="e4m3"):
    dtype, down = {"e4m3": (ml_dtypes.float8_e4m3fn, 7), "e5m2": (ml_dtypes.float8_e5m2, 14)}[fmt]
    v = np.moveaxis(np.asarray(x, np.float32).astype(ml_dtypes.bfloat16).astype(np.float64), axis, -1)
    blocks = v.reshape(v.shape[:-1] + (-1, 32))
    amax = np.abs(blocks).max(-1, keepdims=True)
    byte = np.maximum(np.where(amax > 0, np.frexp(amax)[1] - 1 + 127, 0) - down, 1)
    scale = np.exp2(byte - 127.0)
    codes = (blocks / scale).astype(np.float32).astype(dtype).astype(np.float64)
    return np.moveaxis((codes * scale).reshape(v.shape), -1, axis)


WIDE = False


def mx_kscale(k):
    if not WIDE:
        return np.ones(k)
    levels = np.array([10, -10, 5, -5, 0])
    if k % 512:
        return np.exp2(np.random.permutation(np.resize(levels, k // 32))).repeat(32)
    a = np.empty((k // 512, 16))
    for p in range(k // 512):
        a[p, :8] = np.random.permutation(np.resize(levels, 8))
        for g in range(8):
            far = levels[np.abs(levels - a[p, g]) >= 10]
            a[p, g + 8] = far[np.random.randint(len(far))]
    return np.exp2(a.ravel()).repeat(32)


def f64(x):
    return np.asarray(x).astype(np.float64)


def striped(idx):
    return np.tile(idx.reshape(-1, 16).T, (8, 1)).astype(np.uint16)


def unstriped(offs):
    return offs[:16].T.reshape(-1).astype(np.int64)


def striped8(idx):
    return np.concatenate([x.reshape(-1, 16).T for x in idx]).astype(np.uint16)


def runs(offs, k):
    lists = np.stack([offs[16 * r : 16 * r + 16].T.reshape(-1) for r in range(8)]).astype(np.int64)
    return lists[np.arange(k) % 512 // 64]


def pack_weight(w):
    k, n = w.shape
    w = f64(np.asarray(w, np.float32).astype(ml_dtypes.bfloat16)).reshape(k // 32, 32, n)
    amax = np.abs(w).max(1)
    byte = np.clip(np.where(amax > 0, np.frexp(amax)[1] - 1 + 127 - 7, 1), 1, 254)
    scaled = (w * np.exp2(127.0 - byte)[:, None, :]).reshape(k, n).astype(np.float32)
    words = np.ascontiguousarray(scaled.reshape(k // 512, 128, 4, n).transpose(0, 1, 3, 2)).astype(ml_dtypes.float8_e4m3fn).view(np.uint8)
    return words, np.ascontiguousarray(byte.astype(np.uint8).reshape(k // 512, 16, n))


def unpack_weight(words, scales):
    g, p, n, _ = words.shape
    vals = np.ascontiguousarray(words).view(ml_dtypes.float8_e4m3fn).astype(np.float64) * np.repeat(np.exp2(scales.astype(np.float64) - 127.0), 8, axis=1)[..., None]
    return vals.transpose(0, 1, 3, 2).reshape(g * 512, n)


K, T, S, V, H = 512, 2048, 512, 512, 512


def setup_inputs():
    n = np.random.standard_normal
    s = mx_kscale(K)[:, None]
    packed_xT = pack_weight(n((K, T)) * s)
    return {
        "x_words": packed_xT[0],
        "x_scales": packed_xT[1],
        "w1": (n((K, H)) / np.sqrt(K) / s).astype(np.float32),
        "gs": (np.random.uniform(0.5, 1.5, (K, 1)) / s).astype(np.float32),
        "offs": striped(np.random.permutation(T)[:S]),
        "nb": striped8(np.stack([np.random.permutation(S) for _ in range(8)])),
        "cand": striped(np.random.permutation(T)[:V]),
    }


def reference(x_words, x_scales, w1, gs, offs, nb, cand):
    x_cand = unpack_weight(x_words, x_scales)[:, unstriped(cand)]
    xq = unpack_weight(x_words, x_scales)[:, unstriped(offs)]
    h = mxq(f64(w1), 0, "e4m3").T @ xq
    z = f64(gs) * (h * (h[np.arange(H)[:, None], runs(nb, H)]))
    return 0.0625 * ((x_cand.T @ mxq(z, 0, "e4m3")))

@@ -1,0 +1,168 @@
+from contextlib import ExitStack
+
+import concourse.mybir as mybir
+
+K, T, S, V, H = 512, 2048, 512, 512, 512
+FLOPS = 2 * K * H * S + 2 * K * V * S
+
+F32 = mybir.dt.float32
+BF16 = mybir.dt.bfloat16
+I32 = mybir.dt.int32
+U32 = mybir.dt.uint32
+U16 = mybir.dt.uint16
+U8 = mybir.dt.uint8
+FP8X4 = mybir.dt.float8_e4m3fn_x4
+COPY = mybir.ActivationFunctionType.Copy
+MULT = mybir.AluOpType.mult
+
+P = 128
+PACK = 4
+HALF = S // 2
+OUT_SCALE = 0.0625
+
+
+def tile_picked_candbil_none_p_kernel(tc, x_words, x_scales, w1, gs, offs, nb, cand, out):
+    nc = tc.nc
+    with ExitStack() as ctx:
+        lists = ctx.enter_context(tc.tile_pool(name="lists", bufs=1))
+        sb = ctx.enter_context(tc.tile_pool(name="sb", bufs=1))
+        psum = ctx.enter_context(tc.psum_pool(name="psum", bufs=1))
+
+        def entries(tile, a, b):
+            return tile[:, a // 16 : b // 16]
+
+        offs_t = lists.tile([P, S // 16], U16, name="offs_t")
+        cand_t = lists.tile([P, V // 16], U16, name="cand_t")
+        nb_t = lists.tile([P, S // 16], U16, name="nb_t")
+
+        x_sc = sb.tile([P, T], U8, name="x_sc", align_bytes=64)
+        nc.vector.memset(x_sc[:].bitcast(I32), 0)
+        warm_in = sb.tile([P, 1], F32, name="warm_in")
+        warm_out = sb.tile([P, 1], F32, name="warm_out")
+        nc.vector.memset(warm_in[:], 0.0)
+
+        nc.sync.dma_start(offs_t[:], offs)
+        w_raw = []
+        w_view = w1.rearrange("(p j) c -> p j c", j=PACK)
+        for u in range(2):
+            t_ = sb.tile([P, PACK, H // 2], F32, name=f"w_raw{u}", align_bytes=64)
+            nc.scalar.dma_start(t_[:], w_view[:, :, u * (H // 2) : (u + 1) * (H // 2)])
+            w_raw.append(t_)
+        nc.sync.dma_start(cand_t[:], cand)
+        nc.sync.dma_start(nb_t[:], nb)
+        for q in range(4):
+            nc.sync.dma_start(
+                x_sc[32 * q : 32 * q + 4, :].bitcast(I32), x_scales[0, 4 * q : 4 * q + 4, :].bitcast(I32)
+            )
+        x_w = sb.tile([P, T], U32, name="x_w", align_bytes=64)
+        nc.sync.dma_start(x_w[:].bitcast(I32), x_words[0].rearrange("p n t -> p (n t)").bitcast(I32))
+        gs_t = sb.tile([P, PACK], F32, name="gs_t")
+        nc.gpsimd.dma_start(gs_t[:], gs.rearrange("(p t) o -> p (t o)", t=PACK))
+        nc.scalar.activation(warm_out[:], warm_in[:], COPY)
+
+        xq_sc = sb.tile([P, S], U8, name="xq_sc", align_bytes=64)
+        xc_sc = sb.tile([P, V], U8, name="xc_sc", align_bytes=64)
+        nc.vector.tensor_copy(xq_sc[:], x_sc[:].indirect(offs_t[:]))
+        nc.vector.tensor_copy(xc_sc[:], x_sc[:].indirect(cand_t[:]))
+
+        w_bf = sb.tile([P, PACK, P, PACK], BF16, name="w_bf", align_bytes=64)
+        for u in range(2):
+            nc.scalar.activation(
+                w_bf[:, :, u * 64 : (u + 1) * 64, :].rearrange("p t m j -> p m t j"),
+                w_raw[u][:].rearrange("p j (m t) -> p m t j", t=PACK),
+                COPY,
+            )
+        w_q = sb.tile([P, H], U32, name="w_q", align_bytes=64)
+        w_sc = sb.tile([P, H], U8, name="w_sc", align_bytes=64)
+        nc.vector.quantize_mx(w_q[:].bitcast(FP8X4), w_sc[:], w_bf[:].rearrange("p t m j -> p (t m j)"))
+
+        xq_w = sb.tile([P, S], U32, name="xq_w", align_bytes=64)
+        for a in (0, HALF):
+            nc.vector.tensor_copy(xq_w[:, a : a + HALF], x_w[:].indirect(entries(offs_t, a, a + HALF)))
+        xc_w = sb.tile([P, V], U32, name="xc_w", align_bytes=64)
+        nc.vector.tensor_copy(xc_w[:], x_w[:].indirect(cand_t[:]))
+
+        def first_product(bank, t, a, b):
+            ps = psum.tile([P, b - a], F32, name=f"h_ps{t}_{a}", tag=f"bank{bank}")
+            nc.tensor.matmul_mx(
+                ps[:],
+                lhsT=w_q[:, t * P : (t + 1) * P].bitcast(FP8X4),
+                lhsT_scale=w_sc[:, t * P : (t + 1) * P],
+                rhs=xq_w[:, a:b].bitcast(FP8X4),
+                rhs_scale=xq_sc[:, a:b],
+                start=True,
+                stop=True,
+            )
+            return ps
+
+        h0a = first_product(0, 0, 0, HALF)
+        h0b = first_product(1, 0, HALF, S)
+        h_ps = [None] + [first_product(1 + t, t, 0, S) for t in (1, 2, 3)]
+
+        win = [sb.tile([P, S], F32, name=f"win{t}", align_bytes=64) for t in range(PACK)]
+        own = [sb.tile([P, S], F32, name=f"own{t}", align_bytes=64) for t in range(PACK)]
+        chunks = [(0, 256), (256, 384), (384, 512)]
+        z = [sb.tile([P, PACK, b - a], F32, name=f"z{a}", align_bytes=64) for a, b in chunks]
+
+        def scaled(t, a, b, src):
+            nc.scalar.activation(own[t][:, a:b], src, COPY, scale=gs_t[:, t : t + 1])
+
+        def fetch(t, c):
+            a, b = chunks[c]
+            nc.vector.tensor_tensor(z[c][:, t, :], win[t][:].indirect(entries(nb_t, a, b)), own[t][:, a:b], MULT)
+
+        nc.scalar.activation(win[0][:, 0:HALF], h0a[:], COPY)
+        scaled(0, 0, HALF, h0a[:])
+        nc.scalar.activation(win[0][:, HALF:S], h0b[:], COPY)
+        fetch(0, 0)
+        scaled(0, HALF, S, h0b[:])
+        fetch(0, 1)
+        fetch(0, 2)
+        nc.scalar.activation(win[1][:], h_ps[1][:], COPY)
+        scaled(1, 0, S, h_ps[1][:])
+        for c in range(3):
+            fetch(1, c)
+        for t in (2, 3):
+            nc.scalar.activation(win[t][:], h_ps[t][:], COPY)
+            scaled(t, 0, HALF, h_ps[t][:, 0:HALF])
+            fetch(t, 0)
+        for t in (2, 3):
+            scaled(t, HALF, S, h_ps[t][:, HALF:S])
+        for c in (1, 2):
+            for t in (2, 3):
+                fetch(t, c)
+
+        out_v = out.rearrange("(m p) j -> p m j", p=P)
+        banks = {0: [5, 6], 1: [7], 2: [0, 1]}
+        for c, (a, b) in enumerate(chunks):
+            n = b - a
+            z_bf = sb.tile([P, n, PACK], BF16, name=f"z_bf{c}", align_bytes=64)
+            src = z[c][:].rearrange("p t (g i) -> p g t i", i=4)
+            dst = z_bf[:].rearrange("p (g i) t -> p g t i", i=4)
+            if c == 0:
+                nc.scalar.activation(dst, src, COPY)
+            else:
+                nc.vector.tensor_copy(dst, src)
+            z_q = sb.tile([P, n], U32, name=f"z_q{c}", align_bytes=64)
+            z_sc = sb.tile([P, n], U8, name=f"z_sc{c}", align_bytes=64)
+            nc.vector.quantize_mx(z_q[:].bitcast(FP8X4), z_sc[:], z_bf[:].rearrange("p n t -> p (n t)"))
+            per_bank = 4 // len(banks[c])
+            for g, bank in enumerate(banks[c]):
+                ps = psum.tile([P, per_bank, n], F32, name=f"o_ps{c}_{g}", tag=f"bank{bank}")
+                for i in range(per_bank):
+                    m = g * per_bank + i
+                    nc.tensor.matmul_mx(
+                        ps[:, i, :],
+                        lhsT=xc_w[:, m * P : (m + 1) * P].bitcast(FP8X4),
+                        lhsT_scale=xc_sc[:, m * P : (m + 1) * P],
+                        rhs=z_q[:].bitcast(FP8X4),
+                        rhs_scale=z_sc[:],
+                        start=True,
+                        stop=True,
+                    )
+                res = sb.tile([P, per_bank, n], F32, name=f"res{c}_{g}", align_bytes=64)
+                if c == 2 and g == 1:
+                    nc.vector.tensor_scalar_mul(res[:], ps[:], OUT_SCALE)
+                else:
+                    nc.scalar.activation(res[:], ps[:], COPY, scale=OUT_SCALE)
+                nc.sync.dma_start(out_v[:, g * per_bank : (g + 1) * per_bank, a:b], res[:])

@@ -46,16 +46,17 @@ def tile_picked_candbil_none_p_kernel(tc, x_words, x_scales, w1, gs, offs, nb, c
         w_view = w1.rearrange("(p j) c -> p j c", j=PACK)
         for u in range(2):
             t_ = sb.tile([P, PACK, H // 2], F32, name=f"w_raw{u}", align_bytes=64)
-            nc.scalar.dma_start(t_[:], w_view[:, :, u * (H // 2) : (u + 1) * (H // 2)])
             w_raw.append(t_)
+        nc.scalar.dma_start(w_raw[0][:], w_view[:, :, 0 : H // 2])
         nc.sync.dma_start(cand_t[:], cand)
-        nc.sync.dma_start(nb_t[:], nb)
         for q in range(4):
             nc.sync.dma_start(
                 x_sc[32 * q : 32 * q + 4, :].bitcast(I32), x_scales[0, 4 * q : 4 * q + 4, :].bitcast(I32)
             )
+        nc.sync.dma_start(w_raw[1][:], w_view[:, :, H // 2 : H])
         x_w = sb.tile([P, T], U32, name="x_w", align_bytes=64)
         nc.sync.dma_start(x_w[:].bitcast(I32), x_words[0].rearrange("p n t -> p (n t)").bitcast(I32))
+        nc.sync.dma_start(nb_t[:], nb)
         gs_t = sb.tile([P, PACK], F32, name="gs_t")
         nc.gpsimd.dma_start(gs_t[:], gs.rearrange("(p t) o -> p (t o)", t=PACK))
         nc.scalar.activation(warm_out[:], warm_in[:], COPY)
@@ -96,58 +97,49 @@ def tile_picked_candbil_none_p_kernel(tc, x_words, x_scales, w1, gs, offs, nb, c
             return ps
 
         h0a = first_product(0, 0, 0, HALF)
-        h0b = first_product(1, 0, HALF, S)
+        h0b = first_product(1, 0, 256, 384)
+        h0c = first_product(7, 0, 384, 512)
         h_ps = [None] + [first_product(1 + t, t, 0, S) for t in (1, 2, 3)]
 
         win = [sb.tile([P, S], F32, name=f"win{t}", align_bytes=64) for t in range(PACK)]
-        own = [sb.tile([P, S], F32, name=f"own{t}", align_bytes=64) for t in range(PACK)]
+        own = {}
         chunks = [(0, 256), (256, 384), (384, 512)]
         z = [sb.tile([P, PACK, b - a], F32, name=f"z{a}", align_bytes=64) for a, b in chunks]
 
-        def scaled(t, a, b, src):
-            nc.scalar.activation(own[t][:, a:b], src, COPY, scale=gs_t[:, t : t + 1])
+        def scaled(t, a, b, src, dst=None):
+            if dst is None:
+                piece_tile = sb.tile([P, b - a], F32, name=f"own{t}_{a}", align_bytes=64)
+                dst = piece_tile[:]
+            nc.scalar.activation(dst, src, COPY, scale=gs_t[:, t : t + 1])
+            own[t, a] = dst
 
-        def fetch(t, c):
-            a, b = chunks[c]
-            nc.vector.tensor_tensor(z[c][:, t, :], win[t][:].indirect(entries(nb_t, a, b)), own[t][:, a:b], MULT)
-
-        nc.scalar.activation(win[0][:, 0:HALF], h0a[:], COPY)
-        scaled(0, 0, HALF, h0a[:])
-        nc.scalar.activation(win[0][:, HALF:S], h0b[:], COPY)
-        fetch(0, 0)
-        scaled(0, HALF, S, h0b[:])
-        fetch(0, 1)
-        fetch(0, 2)
-        nc.scalar.activation(win[1][:], h_ps[1][:], COPY)
-        scaled(1, 0, S, h_ps[1][:])
-        for c in range(3):
-            fetch(1, c)
-        for t in (2, 3):
-            nc.scalar.activation(win[t][:], h_ps[t][:], COPY)
-            scaled(t, 0, HALF, h_ps[t][:, 0:HALF])
-            fetch(t, 0)
-        for t in (2, 3):
-            scaled(t, HALF, S, h_ps[t][:, HALF:S])
-        for c in (1, 2):
-            for t in (2, 3):
-                fetch(t, c)
+        def fetch(t, a, b):
+            c = 0 if a < 256 else (a - 128) // 128
+            z0 = chunks[c][0]
+            nc.vector.tensor_tensor(z[c][:, t, a - z0 : b - z0], win[t][:].indirect(entries(nb_t, a, b)), own[t, a], MULT)
 
         out_v = out.rearrange("(m p) j -> p m j", p=P)
-        banks = {0: [5, 6], 1: [7], 2: [0, 1]}
-        for c, (a, b) in enumerate(chunks):
-            n = b - a
-            z_bf = sb.tile([P, n, PACK], BF16, name=f"z_bf{c}", align_bytes=64)
-            src = z[c][:].rearrange("p t (g i) -> p g t i", i=4)
-            dst = z_bf[:].rearrange("p (g i) t -> p g t i", i=4)
-            if c == 0:
+        quarters = [(0, 128), (128, 256), (256, 384), (384, 512)]
+        z_src = [z[0][:, :, 0:128], z[0][:, :, 128:256], z[1][:], z[2][:]]
+        z_bf = [sb.tile([P, b - a, PACK], BF16, name=f"z_bf{a}", align_bytes=64) for a, b in quarters]
+
+        def interleave(c, on_scalar):
+            src = z_src[c].rearrange("p t (g i) -> p g t i", i=4)
+            dst = z_bf[c][:].rearrange("p (g i) t -> p g t i", i=4)
+            if on_scalar:
                 nc.scalar.activation(dst, src, COPY)
             else:
                 nc.vector.tensor_copy(dst, src)
+
+        def second_product(c, banks):
+            a, b = quarters[c]
+            n = b - a
             z_q = sb.tile([P, n], U32, name=f"z_q{c}", align_bytes=64)
             z_sc = sb.tile([P, n], U8, name=f"z_sc{c}", align_bytes=64)
-            nc.vector.quantize_mx(z_q[:].bitcast(FP8X4), z_sc[:], z_bf[:].rearrange("p n t -> p (n t)"))
-            per_bank = 4 // len(banks[c])
-            for g, bank in enumerate(banks[c]):
+            nc.vector.quantize_mx(z_q[:].bitcast(FP8X4), z_sc[:], z_bf[c][:].rearrange("p n t -> p (n t)"))
+            per_bank = 4 // len(banks)
+            tiles = []
+            for g, bank in enumerate(banks):
                 ps = psum.tile([P, per_bank, n], F32, name=f"o_ps{c}_{g}", tag=f"bank{bank}")
                 for i in range(per_bank):
                     m = g * per_bank + i
@@ -160,9 +152,63 @@ def tile_picked_candbil_none_p_kernel(tc, x_words, x_scales, w1, gs, offs, nb, c
                         start=True,
                         stop=True,
                     )
-                res = sb.tile([P, per_bank, n], F32, name=f"res{c}_{g}", align_bytes=64)
-                if c == 2 and g == 1:
-                    nc.vector.tensor_scalar_mul(res[:], ps[:], OUT_SCALE)
-                else:
-                    nc.scalar.activation(res[:], ps[:], COPY, scale=OUT_SCALE)
-                nc.sync.dma_start(out_v[:, g * per_bank : (g + 1) * per_bank, a:b], res[:])
+                tiles.append(ps)
+            return tiles
+
+        def leave(c, g, ps, on_scalar):
+            a, b = quarters[c]
+            per_bank = ps.shape[1]
+            res = sb.tile([P, per_bank, b - a], F32, name=f"res{c}_{g}", align_bytes=64)
+            if on_scalar:
+                nc.scalar.activation(res[:], ps[:], COPY, scale=OUT_SCALE)
+            else:
+                nc.vector.tensor_scalar_mul(res[:], ps[:], OUT_SCALE)
+            nc.sync.dma_start(out_v[:, g * per_bank : (g + 1) * per_bank, a:b], res[:])
+
+        nc.scalar.activation(win[0][:, 0:HALF], h0a[:], COPY)
+        scaled(0, 0, HALF, h0a[:])
+        nc.scalar.activation(win[0][:, 256:384], h0b[:], COPY)
+        nc.scalar.activation(win[0][:, 384:512], h0c[:], COPY)
+        fetch(0, 0, 256)
+        scaled(0, 256, 384, h0b[:])
+        scaled(0, 384, 512, h0c[:])
+        fetch(0, 256, 384)
+        fetch(0, 384, 512)
+        for t in (1, 2):
+            nc.scalar.activation(win[t][:], h_ps[t][:], COPY)
+            scaled(t, 0, HALF, h_ps[t][:, 0:HALF])
+            fetch(t, 0, 256)
+            if t == 1:
+                scaled(1, 256, 384, h_ps[1][:, 256:384])
+                fetch(1, 256, 384)
+        nc.scalar.activation(win[3][:], h_ps[3][:], COPY)
+
+        def piece(t, q, dst=None):
+            a, b = quarters[q]
+            scaled(t, a, b, h_ps[t][:, a:b], dst)
+            fetch(t, a, b)
+
+        first = sb.tile([P, 128], F32, name="own_first", tag="held_a", align_bytes=64)
+        piece(3, 0, first[:])
+        second = sb.tile([P, 128], F32, name="own_second", tag="held_b", align_bytes=64)
+        piece(3, 1, second[:])
+        piece(3, 2)
+        third = sb.tile([P, 128], F32, name="own_third", tag="held_a", align_bytes=64)
+        piece(2, 2, third[:])
+        late = sb.tile([P, 3, 128], F32, name="own_late", tag="held_b", align_bytes=64)
+        interleave(0, True)
+        o_0 = second_product(0, [5])
+        piece(1, 3, late[:, 0, :])
+        interleave(1, True)
+        o_1 = second_product(1, [6])
+        piece(2, 3, late[:, 1, :])
+        interleave(2, True)
+        o_2 = second_product(2, [7])
+        piece(3, 3, late[:, 2, :])
+        interleave(3, False)
+        o_3 = second_product(3, [0, 1, 2, 3])
+        leave(0, 0, o_0[0], True)
+        leave(1, 0, o_1[0], True)
+        leave(2, 0, o_2[0], True)
+        for g in range(4):
+            leave(3, g, o_3[g], g % 2 == 0)

@@ -37,39 +37,39 @@ def tile_picked_candbil_none_p_kernel(tc, x_words, x_scales, w1, gs, offs, nb, c
 
         x_sc = sb.tile([P, T], U8, name="x_sc", align_bytes=64)
         nc.vector.memset(x_sc[:].bitcast(I32), 0)
-        warm_in = sb.tile([P, 1], F32, name="warm_in")
-        warm_out = sb.tile([P, 1], F32, name="warm_out")
-        nc.vector.memset(warm_in[:], 0.0)
+
+        xq_sc = sb.tile([P, S], U8, name="xq_sc", align_bytes=64)
+        xc_sc = sb.tile([P, V], U8, name="xc_sc", align_bytes=64)
+        nc.vector.memset(xq_sc[:].bitcast(I32), 0)
+        nc.vector.memset(xc_sc[:].bitcast(I32), 0)
 
         nc.sync.dma_start(offs_t[:], offs)
-        w_raw = []
         w_view = w1.rearrange("(p j) c -> p j c", j=PACK)
-        for u in range(2):
-            t_ = sb.tile([P, PACK, H // 2], F32, name=f"w_raw{u}", align_bytes=64)
-            w_raw.append(t_)
-        nc.scalar.dma_start(w_raw[0][:], w_view[:, :, 0 : H // 2])
+        w_parts = [(0, 128), (128, 320), (320, 512)]
+        w_raw = [sb.tile([P, PACK, b - a], F32, name=f"w_raw{a}", align_bytes=64) for a, b in w_parts]
+        nc.scalar.dma_start(w_raw[0][:], w_view[:, :, 0:128])
         nc.sync.dma_start(cand_t[:], cand)
-        for q in range(4):
-            nc.sync.dma_start(
-                x_sc[32 * q : 32 * q + 4, :].bitcast(I32), x_scales[0, 4 * q : 4 * q + 4, :].bitcast(I32)
-            )
-        nc.sync.dma_start(w_raw[1][:], w_view[:, :, H // 2 : H])
+        nc.sync.dma_start(x_sc[4:P:8, :].bitcast(I32), x_scales[0].bitcast(I32))
+        for u in (1, 2):
+            nc.sync.dma_start(w_raw[u][:], w_view[:, :, w_parts[u][0] : w_parts[u][1]])
         x_w = sb.tile([P, T], U32, name="x_w", align_bytes=64)
         nc.sync.dma_start(x_w[:].bitcast(I32), x_words[0].rearrange("p n t -> p (n t)").bitcast(I32))
         nc.sync.dma_start(nb_t[:], nb)
         gs_t = sb.tile([P, PACK], F32, name="gs_t")
         nc.gpsimd.dma_start(gs_t[:], gs.rearrange("(p t) o -> p (t o)", t=PACK))
-        nc.scalar.activation(warm_out[:], warm_in[:], COPY)
 
-        xq_sc = sb.tile([P, S], U8, name="xq_sc", align_bytes=64)
-        xc_sc = sb.tile([P, V], U8, name="xc_sc", align_bytes=64)
-        nc.vector.tensor_copy(xq_sc[:], x_sc[:].indirect(offs_t[:]))
-        nc.vector.tensor_copy(xc_sc[:], x_sc[:].indirect(cand_t[:]))
+        for name, picks, plane in (("q", offs_t, xq_sc), ("c", cand_t, xc_sc)):
+            rows = sb.tile([P, S], U8, name=f"rows_{name}", align_bytes=64)
+            nc.vector.tensor_copy(rows[:], x_sc[:].indirect(picks[:]))
+            for q in range(4):
+                nc.sync.dma_start(
+                    plane[32 * q : 32 * q + 4, :].bitcast(I32), rows[32 * q + 4 : 32 * q + 32 : 8, :].bitcast(I32)
+                )
 
         w_bf = sb.tile([P, PACK, P, PACK], BF16, name="w_bf", align_bytes=64)
-        for u in range(2):
+        for u, (a, b) in enumerate(w_parts):
             nc.scalar.activation(
-                w_bf[:, :, u * 64 : (u + 1) * 64, :].rearrange("p t m j -> p m t j"),
+                w_bf[:, :, a // 4 : b // 4, :].rearrange("p t m j -> p m t j"),
                 w_raw[u][:].rearrange("p j (m t) -> p m t j", t=PACK),
                 COPY,
             )

from contextlib import ExitStack

import concourse.mybir as mybir

K, T, S, V, H = 512, 2048, 512, 512, 512
FLOPS = 2 * K * H * S + 2 * K * V * S

F32 = mybir.dt.float32
BF16 = mybir.dt.bfloat16
I32 = mybir.dt.int32
U32 = mybir.dt.uint32
U16 = mybir.dt.uint16
U8 = mybir.dt.uint8
FP8X4 = mybir.dt.float8_e4m3fn_x4
COPY = mybir.ActivationFunctionType.Copy
MULT = mybir.AluOpType.mult

P = 128
PACK = 4
HALF = S // 2
OUT_SCALE = 0.0625


def tile_picked_candbil_none_p_kernel(tc, x_words, x_scales, w1, gs, offs, nb, cand, out):
    nc = tc.nc
    with ExitStack() as ctx:
        lists = ctx.enter_context(tc.tile_pool(name="lists", bufs=1))
        sb = ctx.enter_context(tc.tile_pool(name="sb", bufs=1))
        psum = ctx.enter_context(tc.psum_pool(name="psum", bufs=1))

        def entries(tile, a, b):
            return tile[:, a // 16 : b // 16]

        offs_t = lists.tile([P, S // 16], U16, name="offs_t")
        cand_t = lists.tile([P, V // 16], U16, name="cand_t")
        nb_t = lists.tile([P, S // 16], U16, name="nb_t")

        x_sc = sb.tile([P, T], U8, name="x_sc", align_bytes=64)
        nc.vector.memset(x_sc[:].bitcast(I32), 0)

        xq_sc = sb.tile([P, S], U8, name="xq_sc", align_bytes=64)
        xc_sc = sb.tile([P, V], U8, name="xc_sc", align_bytes=64)
        nc.vector.memset(xq_sc[:].bitcast(I32), 0)
        nc.vector.memset(xc_sc[:].bitcast(I32), 0)

        nc.sync.dma_start(offs_t[:], offs)
        w_view = w1.rearrange("(p j) c -> p j c", j=PACK)
        w_parts = [(0, 128), (128, 320), (320, 512)]
        w_raw = [sb.tile([P, PACK, b - a], F32, name=f"w_raw{a}", align_bytes=64) for a, b in w_parts]
        nc.scalar.dma_start(w_raw[0][:], w_view[:, :, 0:128])
        nc.sync.dma_start(cand_t[:], cand)
        nc.sync.dma_start(x_sc[4:P:8, :].bitcast(I32), x_scales[0].bitcast(I32))
        for u in (1, 2):
            nc.sync.dma_start(w_raw[u][:], w_view[:, :, w_parts[u][0] : w_parts[u][1]])
        x_w = sb.tile([P, T], U32, name="x_w", align_bytes=64)
        nc.sync.dma_start(x_w[:].bitcast(I32), x_words[0].rearrange("p n t -> p (n t)").bitcast(I32))
        nc.sync.dma_start(nb_t[:], nb)
        gs_t = sb.tile([P, PACK], F32, name="gs_t")
        nc.gpsimd.dma_start(gs_t[:], gs.rearrange("(p t) o -> p (t o)", t=PACK))

        for name, picks, plane in (("q", offs_t, xq_sc), ("c", cand_t, xc_sc)):
            rows = sb.tile([P, S], U8, name=f"rows_{name}", align_bytes=64)
            nc.vector.tensor_copy(rows[:], x_sc[:].indirect(picks[:]))
            for q in range(4):
                nc.sync.dma_start(
                    plane[32 * q : 32 * q + 4, :].bitcast(I32), rows[32 * q + 4 : 32 * q + 32 : 8, :].bitcast(I32)
                )

        w_bf = sb.tile([P, PACK, P, PACK], BF16, name="w_bf", align_bytes=64)
        for u, (a, b) in enumerate(w_parts):
            nc.scalar.activation(
                w_bf[:, :, a // 4 : b // 4, :].rearrange("p t m j -> p m t j"),
                w_raw[u][:].rearrange("p j (m t) -> p m t j", t=PACK),
                COPY,
            )
        w_q = sb.tile([P, H], U32, name="w_q", align_bytes=64)
        w_sc = sb.tile([P, H], U8, name="w_sc", align_bytes=64)
        nc.vector.quantize_mx(w_q[:].bitcast(FP8X4), w_sc[:], w_bf[:].rearrange("p t m j -> p (t m j)"))

        xq_w = sb.tile([P, S], U32, name="xq_w", align_bytes=64)
        for a in (0, HALF):
            nc.vector.tensor_copy(xq_w[:, a : a + HALF], x_w[:].indirect(entries(offs_t, a, a + HALF)))
        xc_w = sb.tile([P, V], U32, name="xc_w", align_bytes=64)
        nc.vector.tensor_copy(xc_w[:], x_w[:].indirect(cand_t[:]))

        def first_product(bank, t, a, b):
            ps = psum.tile([P, b - a], F32, name=f"h_ps{t}_{a}", tag=f"bank{bank}")
            nc.tensor.matmul_mx(
                ps[:],
                lhsT=w_q[:, t * P : (t + 1) * P].bitcast(FP8X4),
                lhsT_scale=w_sc[:, t * P : (t + 1) * P],
                rhs=xq_w[:, a:b].bitcast(FP8X4),
                rhs_scale=xq_sc[:, a:b],
                start=True,
                stop=True,
            )
            return ps

        h0a = first_product(0, 0, 0, HALF)
        h0b = first_product(1, 0, 256, 384)
        h0c = first_product(7, 0, 384, 512)
        h_ps = [None] + [first_product(1 + t, t, 0, S) for t in (1, 2, 3)]

        win = [sb.tile([P, S], F32, name=f"win{t}", align_bytes=64) for t in range(PACK)]
        own = {}
        chunks = [(0, 256), (256, 384), (384, 512)]
        z = [sb.tile([P, PACK, b - a], F32, name=f"z{a}", align_bytes=64) for a, b in chunks]

        def scaled(t, a, b, src, dst=None):
            if dst is None:
                piece_tile = sb.tile([P, b - a], F32, name=f"own{t}_{a}", align_bytes=64)
                dst = piece_tile[:]
            nc.scalar.activation(dst, src, COPY, scale=gs_t[:, t : t + 1])
            own[t, a] = dst

        def fetch(t, a, b):
            c = 0 if a < 256 else (a - 128) // 128
            z0 = chunks[c][0]
            nc.vector.tensor_tensor(z[c][:, t, a - z0 : b - z0], win[t][:].indirect(entries(nb_t, a, b)), own[t, a], MULT)

        out_v = out.rearrange("(m p) j -> p m j", p=P)
        quarters = [(0, 128), (128, 256), (256, 384), (384, 512)]
        z_src = [z[0][:, :, 0:128], z[0][:, :, 128:256], z[1][:], z[2][:]]
        z_bf = [sb.tile([P, b - a, PACK], BF16, name=f"z_bf{a}", align_bytes=64) for a, b in quarters]

        def interleave(c, on_scalar):
            src = z_src[c].rearrange("p t (g i) -> p g t i", i=4)
            dst = z_bf[c][:].rearrange("p (g i) t -> p g t i", i=4)
            if on_scalar:
                nc.scalar.activation(dst, src, COPY)
            else:
                nc.vector.tensor_copy(dst, src)

        def second_product(c, banks):
            a, b = quarters[c]
            n = b - a
            z_q = sb.tile([P, n], U32, name=f"z_q{c}", align_bytes=64)
            z_sc = sb.tile([P, n], U8, name=f"z_sc{c}", align_bytes=64)
            nc.vector.quantize_mx(z_q[:].bitcast(FP8X4), z_sc[:], z_bf[c][:].rearrange("p n t -> p (n t)"))
            per_bank = 4 // len(banks)
            tiles = []
            for g, bank in enumerate(banks):
                ps = psum.tile([P, per_bank, n], F32, name=f"o_ps{c}_{g}", tag=f"bank{bank}")
                for i in range(per_bank):
                    m = g * per_bank + i
                    nc.tensor.matmul_mx(
                        ps[:, i, :],
                        lhsT=xc_w[:, m * P : (m + 1) * P].bitcast(FP8X4),
                        lhsT_scale=xc_sc[:, m * P : (m + 1) * P],
                        rhs=z_q[:].bitcast(FP8X4),
                        rhs_scale=z_sc[:],
                        start=True,
                        stop=True,
                    )
                tiles.append(ps)
            return tiles

        def leave(c, g, ps, on_scalar):
            a, b = quarters[c]
            per_bank = ps.shape[1]
            res = sb.tile([P, per_bank, b - a], F32, name=f"res{c}_{g}", align_bytes=64)
            if on_scalar:
                nc.scalar.activation(res[:], ps[:], COPY, scale=OUT_SCALE)
            else:
                nc.vector.tensor_scalar_mul(res[:], ps[:], OUT_SCALE)
            nc.sync.dma_start(out_v[:, g * per_bank : (g + 1) * per_bank, a:b], res[:])

        nc.scalar.activation(win[0][:, 0:HALF], h0a[:], COPY)
        scaled(0, 0, HALF, h0a[:])
        nc.scalar.activation(win[0][:, 256:384], h0b[:], COPY)
        nc.scalar.activation(win[0][:, 384:512], h0c[:], COPY)
        fetch(0, 0, 256)
        scaled(0, 256, 384, h0b[:])
        scaled(0, 384, 512, h0c[:])
        fetch(0, 256, 384)
        fetch(0, 384, 512)
        for t in (1, 2):
            nc.scalar.activation(win[t][:], h_ps[t][:], COPY)
            scaled(t, 0, HALF, h_ps[t][:, 0:HALF])
            fetch(t, 0, 256)
            if t == 1:
                scaled(1, 256, 384, h_ps[1][:, 256:384])
                fetch(1, 256, 384)
        nc.scalar.activation(win[3][:], h_ps[3][:], COPY)

        def piece(t, q, dst=None):
            a, b = quarters[q]
            scaled(t, a, b, h_ps[t][:, a:b], dst)
            fetch(t, a, b)

        first = sb.tile([P, 128], F32, name="own_first", tag="held_a", align_bytes=64)
        piece(3, 0, first[:])
        second = sb.tile([P, 128], F32, name="own_second", tag="held_b", align_bytes=64)
        piece(3, 1, second[:])
        piece(3, 2)
        third = sb.tile([P, 128], F32, name="own_third", tag="held_a", align_bytes=64)
        piece(2, 2, third[:])
        late = sb.tile([P, 3, 128], F32, name="own_late", tag="held_b", align_bytes=64)
        interleave(0, True)
        o_0 = second_product(0, [5])
        piece(1, 3, late[:, 0, :])
        interleave(1, True)
        o_1 = second_product(1, [6])
        piece(2, 3, late[:, 1, :])
        interleave(2, True)
        o_2 = second_product(2, [7])
        piece(3, 3, late[:, 2, :])
        interleave(3, False)
        o_3 = second_product(3, [0, 1, 2, 3])
        leave(0, 0, o_0[0], True)
        leave(1, 0, o_1[0], True)
        leave(2, 0, o_2[0], True)
        for g in range(4):
            leave(3, g, o_3[g], g % 2 == 0)
